import numpy as np
import ml_dtypes


def mxq(x, axis, fmt="e4m3"):
    dtype, down = {"e4m3": (ml_dtypes.float8_e4m3fn, 7), "e5m2": (ml_dtypes.float8_e5m2, 14)}[fmt]
    v = np.moveaxis(np.asarray(x, np.float32).astype(ml_dtypes.bfloat16).astype(np.float64), axis, -1)
    blocks = v.reshape(v.shape[:-1] + (-1, 32))
    amax = np.abs(blocks).max(-1, keepdims=True)
    byte = np.maximum(np.where(amax > 0, np.frexp(amax)[1] - 1 + 127, 0) - down, 1)
    scale = np.exp2(byte - 127.0)
    codes = (blocks / scale).astype(np.float32).astype(dtype).astype(np.float64)
    return np.moveaxis((codes * scale).reshape(v.shape), -1, axis)


WIDE = False


def mx_kscale(k, group=512):
    if not WIDE:
        return np.ones(k)
    levels = np.array([18, -18])
    if group != 512:
        return np.exp2(np.random.permutation(np.resize(levels, k // group))).repeat(group)
    if k % 512:
        return np.exp2(np.random.permutation(np.resize(levels, k // 32))).repeat(32)
    a = np.empty((k // 512, 16))
    for p in range(k // 512):
        a[p, :8] = np.random.permutation(np.resize(levels, 8))
        for g in range(8):
            far = levels[np.abs(levels - a[p, g]) >= 10]
            a[p, g + 8] = far[np.random.randint(len(far))]
    return np.exp2(a.ravel()).repeat(32)


def f64(x):
    return np.asarray(x).astype(np.float64)


def bf(x):
    return np.asarray(x, np.float32).astype(ml_dtypes.bfloat16)


def planes(Y):
    r, m = Y.shape
    b = f64(bf(Y)).reshape(r // 32, 32, m)
    amax = np.abs(b).max(1)
    byte = np.clip(np.where(amax > 0, np.frexp(amax)[1] - 1 + 127 - 7, 1), 1, 254)
    codes = (b * np.exp2(127.0 - byte)[:, None, :]).reshape(r, m).astype(np.float32).astype(ml_dtypes.float8_e4m3fn).view(np.uint8)
    words = codes.reshape(r // 512, 128, 4, m).transpose(0, 1, 3, 2)
    return np.ascontiguousarray(words), np.ascontiguousarray(byte.astype(np.uint8).reshape(r // 512, 16, m))


G, D, M, N = 4, 128, 128, 512


def setup_inputs():
    n = np.random.standard_normal
    s_d = mx_kscale(D, 0)
    return {
        "x": (n((G, D, N)) * s_d[:, None]).astype(np.float32),
        "fc": (np.cos(2 * np.pi * np.outer(np.arange(D), np.arange(M)) / D) * (2 / np.sqrt(D)) / s_d[:, None]).astype(np.float32),
        "fs": (np.sin(2 * np.pi * (np.outer(np.arange(D), np.arange(M)) + 0.25) / D) * (2 / np.sqrt(D)) / s_d[:, None]).astype(np.float32),
        "nz": (np.random.uniform(0.5, 2.0, (G, M, 1))).astype(np.float32),
    }


def reference(x, fc, fs, nz):
    fcq = mxq(f64(fc), 0, "e4m3")
    xq = mxq(f64(x), 1, "e4m3")
    re = fcq.T @ xq
    fsq = mxq(f64(fs), 0, "e4m3")
    im = fsq.T @ xq
    pw = np.square(re) + np.square(im)
    y = pw / (pw + f64(nz))
    Y = y.reshape(G * M, N)
    words, scales = planes(Y)
    return Y, words, scales

@@ -1,0 +1,214 @@
+from contextlib import ExitStack
+
+import concourse.mybir as mybir
+
+G, D, M, N = 4, 128, 128, 512
+FLOPS = 2 * 2 * G * D * M * N
+
+F32 = mybir.dt.float32
+BF16 = mybir.dt.bfloat16
+I32 = mybir.dt.int32
+U8 = mybir.dt.uint8
+FP8X4 = mybir.dt.float8_e4m3fn_x4
+ACT = mybir.ActivationFunctionType
+ALU = mybir.AluOpType
+
+P = 128
+PACK = 4
+ROWS = 32
+HALF = 256
+MM_N = 128
+CHUNKS = [(0, 256), (256, 128), (384, 128)]
+
+
+def interleave(copy, dst, src):
+    copy(
+        out=dst.rearrange("p (c i) t -> p c t i", i=4),
+        in_=src.rearrange("p t (c i) -> p c t i", i=4),
+    )
+
+
+def quantise(nc, codes, scales, grouped):
+    nc.vector.quantize_mx(
+        out=codes.bitcast(FP8X4),
+        scales=scales,
+        in_=grouped.rearrange("p n t -> p (n t)"),
+    )
+
+
+def tile_rows_pl_dft_wiener_kernel(tc, x, fc, fs, nz, out_0, out_1, out_2):
+    nc = tc.nc
+    with ExitStack() as ctx:
+        sb = ctx.enter_context(tc.tile_pool(name="sb", bufs=1))
+        psum = ctx.enter_context(tc.psum_pool(name="psum", bufs=1))
+        ctx.enter_context(tc.manual_schedule())
+
+        def tile(name, shape, dtype):
+            return sb.tile(shape, dtype, name=name, align_bytes=64)
+
+        f_raw = [[tile("f_raw%d" % s, [2 * ROWS, PACK, M], F32)] for s in range(2)]
+        f_raw = [t[0] for t in f_raw]
+        for s, (eng, f) in enumerate(((nc.sync, fc), (nc.scalar, fs))):
+            for q in range(2):
+                eng.dma_start(
+                    out=f_raw[s][ROWS * q : ROWS * (q + 1)],
+                    in_=f.rearrange("(p j) m -> p j m", j=PACK),
+                )
+        x_rows = x.rearrange("g (p j) n -> (g p) j n", j=PACK)
+        x_raw = []
+        for h in range(2):
+            t = tile("x_raw%d" % h, [P, PACK, HALF], F32)
+            nc.sync.dma_start(out=t[:], in_=x_rows[:, :, HALF * h : HALF * (h + 1)])
+            x_raw.append(t)
+        noise = tile("noise", [P, G], F32)
+        with nc.allow_non_contiguous_dma(reason="one noise value for each bin and channel"):
+            nc.sync.dma_start(out=noise[:], in_=nz.rearrange("g m o -> m (g o)"))
+
+        w = tile("w", [P, 2 * M + 2 * M // 4], I32)
+        w_codes = w[:, 0 : 2 * M]
+        w_scales = w[:, 2 * M :].bitcast(U8)
+        one = tile("one", [P, 1], F32)
+        warm = tile("warm", [P, 1], F32)
+        nc.gpsimd.memset(one[:], 1.0)
+        nc.gpsimd.memset(w[:, 2 * M :], 0)
+        nc.scalar.activation(out=warm[:], in_=one[:], func=ACT.Abs_reciprocal_sqrt)
+
+        f_grp = [tile("f_grp%d" % s, [2 * ROWS, M, PACK], BF16) for s in range(2)]
+        interleave(nc.vector.tensor_copy, f_grp[0][:], f_raw[0][:])
+        interleave(nc.scalar.copy, f_grp[1][:], f_raw[1][:])
+        for s in range(2):
+            cols = slice(M * s, M * (s + 1))
+            quantise(nc, w_codes[0 : 2 * ROWS, cols], w_scales[0 : 2 * ROWS, cols], f_grp[s][:])
+        nc.sync.dma_start(out=w[2 * ROWS :, :], in_=w[0 : 2 * ROWS, :])
+
+        x_codes = [tile("x_codes%d" % c, [P, MM_N], I32) for c in range(4)]
+        x_scales = [tile("x_scales%d" % c, [P, MM_N], U8) for c in range(4)]
+        x_grp = [tile("x_grp%d" % c, [P, MM_N, PACK], BF16) for c in range(4)]
+
+        def round_x(copy, c):
+            interleave(copy, x_grp[c][:], x_raw[c // 2][:, :, MM_N * (c % 2) : MM_N * (c % 2 + 1)])
+
+        def quantise_x(c):
+            quantise(nc, x_codes[c][:], x_scales[c][:], x_grp[c][:])
+
+        round_x(nc.vector.tensor_copy, 0)
+        round_x(nc.scalar.copy, 1)
+        quantise_x(0)
+        quantise_x(1)
+        round_x(nc.vector.tensor_copy, 2)
+        round_x(nc.vector.tensor_copy, 3)
+        quantise_x(2)
+        quantise_x(3)
+
+        spec = [[psum.tile([P, 2, HALF], F32, name="spec%d_%d" % (g, h)) for h in range(2)] for g in range(G)]
+
+        def spectra(h, groups):
+            for i in range(2):
+                c = 2 * h + i
+                for s in range(2):
+                    for g in groups:
+                        rows = slice(ROWS * g, ROWS * (g + 1))
+                        cols = slice(M * s, M * (s + 1))
+                        nc.tensor.matmul_mx(
+                            out=spec[g][h][:, s, MM_N * i : MM_N * (i + 1)],
+                            lhsT=w_codes[rows, cols].bitcast(FP8X4),
+                            lhsT_scale=w_scales[rows, cols],
+                            rhs=x_codes[c][rows, :].bitcast(FP8X4),
+                            rhs_scale=x_scales[c][rows, :],
+                            start=True,
+                            stop=True,
+                        )
+
+        spectra(0, (0, 1))
+        spectra(0, (2, 3))
+        spectra(1, (0, 1, 2, 3))
+
+        stages = [(0, (g,)) for g in range(G)] + [(c, gs) for c in (1, 2) for gs in ((0, 1), (2, 3))]
+        gain = [tile("gain%d" % c, [P, G, wd], F32) for c, (n0, wd) in enumerate(CHUNKS)]
+        dealt = [tile("dealt%d" % c, [P, PACK, wd], F32) for c, (n0, wd) in enumerate(CHUNKS)]
+        sq, pw, rs, part = [], [], [], []
+        for i, (c, gs) in enumerate(stages):
+            wd = CHUNKS[c][1]
+            sq.append(tile("sq%d" % i, [P, 2, len(gs), wd], F32))
+            pw.append(tile("pw%d" % i, [P, len(gs), wd], F32))
+            rs.append(tile("rs%d" % i, [P, len(gs), wd], F32))
+            part.append(tile("part%d" % i, [P, len(gs), wd], F32))
+        out_rows = out_0.rearrange("(g m) n -> m g n", g=G)
+
+        def squares(i):
+            c, gs = stages[i]
+            n0, wd = CHUNKS[c]
+            for k, g in enumerate(gs):
+                nc.scalar.activation(
+                    out=sq[i][:, :, k, :],
+                    in_=spec[g][n0 // HALF][:, :, n0 % HALF : n0 % HALF + wd],
+                    func=ACT.Square,
+                )
+
+        def power(i):
+            nc.vector.tensor_tensor(out=pw[i][:], in0=sq[i][:, 0], in1=sq[i][:, 1], op=ALU.add)
+
+        def root(i):
+            for k, g in enumerate(stages[i][1]):
+                nc.scalar.activation(
+                    out=rs[i][:, k, :], in_=pw[i][:, k, :], func=ACT.Abs_reciprocal_sqrt, bias=noise[:, g : g + 1]
+                )
+
+        def first_product(i, ks):
+            nc.vector.tensor_tensor(out=part[i][:, ks], in0=pw[i][:, ks], in1=rs[i][:, ks], op=ALU.mult)
+
+        def second_product(i, ks):
+            c, gs = stages[i]
+            gsel = gs[ks]
+            nc.vector.tensor_tensor(
+                out=gain[c][:, gsel[0] : gsel[-1] + 1], in0=part[i][:, ks], in1=rs[i][:, ks], op=ALU.mult
+            )
+            for g in gsel:
+                nc.sync.dma_start(out=dealt[c][ROWS * g : ROWS * (g + 1)], in_=gain[c][:, g, :])
+            if gsel[-1] == G - 1:
+                n0, wd = CHUNKS[c]
+                nc.sync.dma_start(out=out_rows[:, :, n0 : n0 + wd], in_=gain[c][:])
+
+        last = len(stages) - 1
+        whole = slice(None)
+        squares(0)
+        squares(1)
+        power(0)
+        power(1)
+        for i in range(last):
+            root(i)
+            first_product(i, whole)
+            if i + 2 <= last:
+                squares(i + 2)
+                power(i + 2)
+            second_product(i, whole)
+        root(last)
+        first_product(last, slice(0, 1))
+        first_product(last, slice(1, 2))
+        second_product(last, slice(0, 1))
+        second_product(last, slice(1, 2))
+
+        words = tile("words", [P, N], I32)
+        scales = tile("scales", [P, N], U8)
+        y_grp = [tile("y_grp%d" % c, [P, wd, PACK], BF16) for c, (n0, wd) in enumerate(CHUNKS)]
+        word_rows = out_1.rearrange("v p n t -> (v p) (n t)").bitcast(I32)
+        scale_rows = out_2.rearrange("v f n -> (v f) n").bitcast(I32)
+
+        def quantise_y(c):
+            n0, wd = CHUNKS[c]
+            quantise(nc, words[:, n0 : n0 + wd], scales[:, n0 : n0 + wd], y_grp[c][:])
+
+        interleave(nc.vector.tensor_copy, y_grp[0][:], dealt[0][:])
+        interleave(nc.scalar.copy, y_grp[1][:], dealt[1][:])
+        quantise_y(0)
+        quantise_y(1)
+        nc.sync.dma_start(out=word_rows[:, 0:384], in_=words[:, 0:384])
+        interleave(nc.vector.tensor_copy, y_grp[2][:], dealt[2][:])
+        quantise_y(2)
+        nc.sync.dma_start(out=word_rows[:, 384:], in_=words[:, 384:])
+        for q in range(4):
+            eng = nc.scalar if q % 2 == 0 else nc.sync
+            eng.dma_start(
+                out=scale_rows[4 * q : 4 * q + 4, :],
+                in_=scales[:].bitcast(I32)[ROWS * q : ROWS * q + 4, :],
+            )

@@ -16,9 +16,12 @@ ALU = mybir.AluOpType
 P = 128
 PACK = 4
 ROWS = 32
-HALF = 256
-MM_N = 128
-CHUNKS = [(0, 256), (256, 128), (384, 128)]
+CH = 128
+CHUNKS = N // CH
+PAIRS = ((0, 2), (1, 3))
+SCALAR_SQUARES = ()
+TAIL = 128
+VECTOR_COLS = 80
 
 
 def interleave(copy, dst, src):
@@ -36,6 +39,10 @@ def quantise(nc, codes, scales, grouped):
     )
 
 
+def quadrant(q):
+    return slice(ROWS * q, ROWS * (q + 1))
+
+
 def tile_rows_pl_dft_wiener_kernel(tc, x, fc, fs, nz, out_0, out_1, out_2):
     nc = tc.nc
     with ExitStack() as ctx:
@@ -46,168 +53,194 @@ def tile_rows_pl_dft_wiener_kernel(tc, x, fc, fs, nz, out_0, out_1, out_2):
         def tile(name, shape, dtype):
             return sb.tile(shape, dtype, name=name, align_bytes=64)
 
-        f_raw = [[tile("f_raw%d" % s, [2 * ROWS, PACK, M], F32)] for s in range(2)]
-        f_raw = [t[0] for t in f_raw]
-        for s, (eng, f) in enumerate(((nc.sync, fc), (nc.scalar, fs))):
-            for q in range(2):
-                eng.dma_start(
-                    out=f_raw[s][ROWS * q : ROWS * (q + 1)],
-                    in_=f.rearrange("(p j) m -> p j m", j=PACK),
-                )
-        x_rows = x.rearrange("g (p j) n -> (g p) j n", j=PACK)
-        x_raw = []
-        for h in range(2):
-            t = tile("x_raw%d" % h, [P, PACK, HALF], F32)
-            nc.sync.dma_start(out=t[:], in_=x_rows[:, :, HALF * h : HALF * (h + 1)])
-            x_raw.append(t)
-        noise = tile("noise", [P, G], F32)
-        with nc.allow_non_contiguous_dma(reason="one noise value for each bin and channel"):
-            nc.sync.dma_start(out=noise[:], in_=nz.rearrange("g m o -> m (g o)"))
-
+        f_raw = [tile("f_raw%d" % s, [P, PACK, M], F32) for s in range(2)]
+        noise_rows = tile("noise_rows", [P, G * ROWS], F32)
+        noise = tile("noise", [P, G * ROWS], F32)
         w = tile("w", [P, 2 * M + 2 * M // 4], I32)
         w_codes = w[:, 0 : 2 * M]
         w_scales = w[:, 2 * M :].bitcast(U8)
         one = tile("one", [P, 1], F32)
         warm = tile("warm", [P, 1], F32)
+        nc.gpsimd.memset(noise_rows[:], 0.0)
         nc.gpsimd.memset(one[:], 1.0)
         nc.gpsimd.memset(w[:, 2 * M :], 0)
+        for s in range(2):
+            for q in PAIRS[1]:
+                nc.vector.memset(f_raw[s][quadrant(q)], 0.0)
+
+        for eng, f, raw in ((nc.sync, fc, f_raw[0]), (nc.scalar, fs, f_raw[1])):
+            for q in PAIRS[0]:
+                eng.dma_start(out=raw[quadrant(q)], in_=f.rearrange("(p j) m -> p j m", j=PACK))
+        x_rows = x.rearrange("g (p j) n -> (g p) j n", j=PACK)
+        x_raw = []
+
+        def load_x(c0, c1):
+            t = tile("x_raw%d" % c0, [P, PACK, CH * (c1 - c0)], F32)
+            nc.sync.dma_start(out=t[:], in_=x_rows[:, :, CH * c0 : CH * c1])
+            x_raw.extend(t[:, :, CH * k : CH * (k + 1)] for k in range(c1 - c0))
+
+        load_x(0, 1)
+        nc.sync.dma_start(
+            out=noise_rows[0:P:ROWS, :].rearrange("q (g i) -> q g i", g=G),
+            in_=nz.rearrange("g (q i) o -> q g (i o)", i=ROWS),
+        )
+        load_x(1, 2)
+        load_x(2, 4)
         nc.scalar.activation(out=warm[:], in_=one[:], func=ACT.Abs_reciprocal_sqrt)
 
-        f_grp = [tile("f_grp%d" % s, [2 * ROWS, M, PACK], BF16) for s in range(2)]
-        interleave(nc.vector.tensor_copy, f_grp[0][:], f_raw[0][:])
-        interleave(nc.scalar.copy, f_grp[1][:], f_raw[1][:])
-        for s in range(2):
-            cols = slice(M * s, M * (s + 1))
-            quantise(nc, w_codes[0 : 2 * ROWS, cols], w_scales[0 : 2 * ROWS, cols], f_grp[s][:])
-        nc.sync.dma_start(out=w[2 * ROWS :, :], in_=w[0 : 2 * ROWS, :])
+        f_grp = [tile("f_grp%d" % s, [P, M, PACK], BF16) for s in range(2)]
+        x_codes = [tile("x_codes%d" % c, [P, CH], I32) for c in range(CHUNKS)]
+        x_scales = [tile("x_scales%d" % c, [P, CH], U8) for c in range(CHUNKS)]
+        x_grp = [tile("x_grp%d" % c, [P, CH, PACK], BF16) for c in range(CHUNKS)]
 
-        x_codes = [tile("x_codes%d" % c, [P, MM_N], I32) for c in range(4)]
-        x_scales = [tile("x_scales%d" % c, [P, MM_N], U8) for c in range(4)]
-        x_grp = [tile("x_grp%d" % c, [P, MM_N, PACK], BF16) for c in range(4)]
-
-        def round_x(copy, c):
-            interleave(copy, x_grp[c][:], x_raw[c // 2][:, :, MM_N * (c % 2) : MM_N * (c % 2 + 1)])
+        def round_x(copy, c, lo=0, hi=CH):
+            interleave(copy, x_grp[c][:, lo:hi], x_raw[c][:, :, lo:hi])
 
         def quantise_x(c):
             quantise(nc, x_codes[c][:], x_scales[c][:], x_grp[c][:])
 
-        round_x(nc.vector.tensor_copy, 0)
-        round_x(nc.scalar.copy, 1)
+        def quantise_f(s):
+            cols = slice(M * s, M * (s + 1))
+            quantise(nc, w_codes[:, cols], w_scales[:, cols], f_grp[s][:])
+
+        interleave(nc.vector.tensor_copy, f_grp[0][:], f_raw[0][:])
+        interleave(nc.scalar.copy, f_grp[1][:], f_raw[1][:])
+        quantise_f(0)
+        round_x(nc.vector.tensor_copy, 0, 0, VECTOR_COLS)
+        round_x(nc.scalar.copy, 0, VECTOR_COLS, CH)
+        quantise_f(1)
         quantise_x(0)
+        for src, dst in zip(*PAIRS):
+            nc.scalar.dma_start(out=w[quadrant(dst), :], in_=w[quadrant(src), :])
+        round_x(nc.vector.tensor_copy, 1, 0, VECTOR_COLS)
+        round_x(nc.scalar.copy, 1, VECTOR_COLS, CH)
+        nc.vector.transpose(out=noise[:], in_=noise_rows[:])
         quantise_x(1)
-        round_x(nc.vector.tensor_copy, 2)
-        round_x(nc.vector.tensor_copy, 3)
-        quantise_x(2)
-        quantise_x(3)
 
-        spec = [[psum.tile([P, 2, HALF], F32, name="spec%d_%d" % (g, h)) for h in range(2)] for g in range(G)]
+        spec = [[psum.tile([P, 2, 2, CH], F32, name="spec%d_%d" % (g, b)) for b in range(2)] for g in range(G)]
 
-        def spectra(h, groups):
-            for i in range(2):
-                c = 2 * h + i
-                for s in range(2):
-                    for g in groups:
-                        rows = slice(ROWS * g, ROWS * (g + 1))
-                        cols = slice(M * s, M * (s + 1))
-                        nc.tensor.matmul_mx(
-                            out=spec[g][h][:, s, MM_N * i : MM_N * (i + 1)],
-                            lhsT=w_codes[rows, cols].bitcast(FP8X4),
-                            lhsT_scale=w_scales[rows, cols],
-                            rhs=x_codes[c][rows, :].bitcast(FP8X4),
-                            rhs_scale=x_scales[c][rows, :],
-                            start=True,
-                            stop=True,
-                        )
+        def spectra(c, groups):
+            for s in range(2):
+                for g in groups:
+                    cols = slice(M * s, M * (s + 1))
+                    nc.tensor.matmul_mx(
+                        out=spec[g][c % 2][:, c // 2, s, :],
+                        lhsT=w_codes[quadrant(g), cols].bitcast(FP8X4),
+                        lhsT_scale=w_scales[quadrant(g), cols],
+                        rhs=x_codes[c][quadrant(g), :].bitcast(FP8X4),
+                        rhs_scale=x_scales[c][quadrant(g), :],
+                        start=True,
+                        stop=True,
+                    )
 
-        spectra(0, (0, 1))
-        spectra(0, (2, 3))
-        spectra(1, (0, 1, 2, 3))
+        every = tuple(range(G))
+        stages = [(CH * c, CH, gs) for gs in PAIRS for c in (0, 1)]
+        stages += [(2 * CH, CH, gs) for gs in PAIRS]
+        stages += [(3 * CH, CH - TAIL, every)] if TAIL == 64 else []
+        stages += [(N - TAIL, TAIL, gs) for gs in PAIRS]
+        for n0, wd, gs in stages[:4]:
+            spectra(n0 // CH, gs)
 
-        stages = [(0, (g,)) for g in range(G)] + [(c, gs) for c in (1, 2) for gs in ((0, 1), (2, 3))]
-        gain = [tile("gain%d" % c, [P, G, wd], F32) for c, (n0, wd) in enumerate(CHUNKS)]
-        dealt = [tile("dealt%d" % c, [P, PACK, wd], F32) for c, (n0, wd) in enumerate(CHUNKS)]
-        sq, pw, rs, part = [], [], [], []
-        for i, (c, gs) in enumerate(stages):
-            wd = CHUNKS[c][1]
-            sq.append(tile("sq%d" % i, [P, 2, len(gs), wd], F32))
-            pw.append(tile("pw%d" % i, [P, len(gs), wd], F32))
-            rs.append(tile("rs%d" % i, [P, len(gs), wd], F32))
-            part.append(tile("part%d" % i, [P, len(gs), wd], F32))
+        blocks = ((0, 2 * CH), (2 * CH, 2 * CH - TAIL), (N - TAIL, TAIL))
+        gain = [tile("gain%d" % h, [P, G, 2 * CH], F32) for h in range(2)]
+        dealt = [tile("dealt%d" % b, [P, PACK, wd], F32) for b, (n0, wd) in enumerate(blocks)]
+        sq = [tile("sq%d" % i, [P, 2, len(gs), wd], F32) for i, (n0, wd, gs) in enumerate(stages)]
+        pw = [tile("pw%d" % i, [P, len(gs), wd], F32) for i, (n0, wd, gs) in enumerate(stages)]
+        rs = [tile("rs%d" % i, [P, len(gs), wd], F32) for i, (n0, wd, gs) in enumerate(stages)]
+        part = [tile("part%d" % i, [P, len(gs), wd], F32) for i, (n0, wd, gs) in enumerate(stages)]
         out_rows = out_0.rearrange("(g m) n -> m g n", g=G)
 
         def squares(i):
-            c, gs = stages[i]
-            n0, wd = CHUNKS[c]
-            for k, g in enumerate(gs):
+            n0, wd, gs = stages[i]
+            c, lo = divmod(n0, CH)
+            for j, g in enumerate(gs):
                 nc.scalar.activation(
-                    out=sq[i][:, :, k, :],
-                    in_=spec[g][n0 // HALF][:, :, n0 % HALF : n0 % HALF + wd],
-                    func=ACT.Square,
+                    out=sq[i][:, :, j, :], in_=spec[g][c % 2][:, c // 2, :, lo : lo + wd], func=ACT.Square
                 )
 
         def power(i):
             nc.vector.tensor_tensor(out=pw[i][:], in0=sq[i][:, 0], in1=sq[i][:, 1], op=ALU.add)
 
         def root(i):
-            for k, g in enumerate(stages[i][1]):
+            for j, g in enumerate(stages[i][2]):
                 nc.scalar.activation(
-                    out=rs[i][:, k, :], in_=pw[i][:, k, :], func=ACT.Abs_reciprocal_sqrt, bias=noise[:, g : g + 1]
+                    out=rs[i][:, j, :],
+                    in_=pw[i][:, j, :],
+                    func=ACT.Abs_reciprocal_sqrt,
+                    bias=noise[:, ROWS * g : ROWS * g + 1],
                 )
 
-        def first_product(i, ks):
-            nc.vector.tensor_tensor(out=part[i][:, ks], in0=pw[i][:, ks], in1=rs[i][:, ks], op=ALU.mult)
+        def first_product(i):
+            if i in SCALAR_SQUARES:
+                nc.scalar.activation(out=part[i][:], in_=rs[i][:], func=ACT.Square)
+            else:
+                nc.vector.tensor_tensor(out=part[i][:], in0=pw[i][:], in1=rs[i][:], op=ALU.mult)
 
-        def second_product(i, ks):
-            c, gs = stages[i]
-            gsel = gs[ks]
-            nc.vector.tensor_tensor(
-                out=gain[c][:, gsel[0] : gsel[-1] + 1], in0=part[i][:, ks], in1=rs[i][:, ks], op=ALU.mult
-            )
-            for g in gsel:
-                nc.sync.dma_start(out=dealt[c][ROWS * g : ROWS * (g + 1)], in_=gain[c][:, g, :])
-            if gsel[-1] == G - 1:
-                n0, wd = CHUNKS[c]
-                nc.sync.dma_start(out=out_rows[:, :, n0 : n0 + wd], in_=gain[c][:])
+        def second_product(i):
+            n0, wd, gs = stages[i]
+            h, lo = divmod(n0, 2 * CH)
+            sel = slice(gs[0], G, gs[1] - gs[0])
+            other = pw[i] if i in SCALAR_SQUARES else rs[i]
+            nc.vector.tensor_tensor(out=gain[h][:, sel, lo : lo + wd], in0=part[i][:], in1=other[:], op=ALU.mult)
+            for b, (b0, bw) in enumerate(blocks):
+                if n0 + wd == b0 + bw:
+                    for g in gs:
+                        nc.sync.dma_start(
+                            out=dealt[b][quadrant(g)], in_=gain[h][:, g, b0 % (2 * CH) : b0 % (2 * CH) + bw]
+                        )
+            if n0 == CH:
+                nc.sync.dma_start(out=out_rows[:, sel, 0 : 2 * CH], in_=gain[0][:, sel, :])
 
         last = len(stages) - 1
-        whole = slice(None)
         squares(0)
         squares(1)
         power(0)
+        round_x(nc.vector.tensor_copy, 2)
         power(1)
-        for i in range(last):
+        quantise_x(2)
+        for i in range(last - 1):
             root(i)
-            first_product(i, whole)
-            if i + 2 <= last:
-                squares(i + 2)
-                power(i + 2)
-            second_product(i, whole)
+            squares(i + 2)
+            first_product(i)
+            if i == 0:
+                round_x(nc.vector.tensor_copy, 3)
+                spectra(2, every)
+            power(i + 2)
+            second_product(i)
+            if i == 0:
+                quantise_x(3)
+            if i == 1:
+                spectra(3, every)
+        root(last - 1)
+        first_product(last - 1)
         root(last)
-        first_product(last, slice(0, 1))
-        first_product(last, slice(1, 2))
-        second_product(last, slice(0, 1))
-        second_product(last, slice(1, 2))
+        first_product(last)
+        second_product(last - 1)
+        second_product(last)
+        nc.sync.dma_start(out=out_rows[:, :, 2 * CH :], in_=gain[1][:])
 
         words = tile("words", [P, N], I32)
         scales = tile("scales", [P, N], U8)
-        y_grp = [tile("y_grp%d" % c, [P, wd, PACK], BF16) for c, (n0, wd) in enumerate(CHUNKS)]
+        y_grp = [tile("y_grp%d" % b, [P, wd, PACK], BF16) for b, (n0, wd) in enumerate(blocks)]
         word_rows = out_1.rearrange("v p n t -> (v p) (n t)").bitcast(I32)
         scale_rows = out_2.rearrange("v f n -> (v f) n").bitcast(I32)
 
-        def quantise_y(c):
-            n0, wd = CHUNKS[c]
-            quantise(nc, words[:, n0 : n0 + wd], scales[:, n0 : n0 + wd], y_grp[c][:])
+        def quantise_y(b, lo, hi):
+            n0 = blocks[b][0]
+            quantise(nc, words[:, n0 + lo : n0 + hi], scales[:, n0 + lo : n0 + hi], y_grp[b][:, lo:hi])
 
         interleave(nc.vector.tensor_copy, y_grp[0][:], dealt[0][:])
         interleave(nc.scalar.copy, y_grp[1][:], dealt[1][:])
-        quantise_y(0)
-        quantise_y(1)
-        nc.sync.dma_start(out=word_rows[:, 0:384], in_=words[:, 0:384])
+        quantise_y(0, 0, 2 * CH)
+        quantise_y(1, 0, CH)
+        if TAIL < CH:
+            quantise_y(1, CH, 2 * CH - TAIL)
+        nc.sync.dma_start(out=word_rows[:, 0 : N - TAIL], in_=words[:, 0 : N - TAIL])
         interleave(nc.vector.tensor_copy, y_grp[2][:], dealt[2][:])
-        quantise_y(2)
-        nc.sync.dma_start(out=word_rows[:, 384:], in_=words[:, 384:])
+        quantise_y(2, 0, TAIL)
+        nc.scalar.dma_start(out=word_rows[:, N - TAIL :], in_=words[:, N - TAIL :])
         for q in range(4):
-            eng = nc.scalar if q % 2 == 0 else nc.sync
+            eng = nc.sync if q % 2 == 0 else nc.scalar
             eng.dma_start(
                 out=scale_rows[4 * q : 4 * q + 4, :],
                 in_=scales[:].bitcast(I32)[ROWS * q : ROWS * q + 4, :],

@@ -19,9 +19,8 @@ ROWS = 32
 CH = 128
 CHUNKS = N // CH
 PAIRS = ((0, 2), (1, 3))
-SCALAR_SQUARES = ()
-TAIL = 128
 VECTOR_COLS = 80
+MOVED_AS_POWER = (1, 2)
 
 
 def interleave(copy, dst, src):
@@ -86,6 +85,8 @@ def tile_rows_pl_dft_wiener_kernel(tc, x, fc, fs, nz, out_0, out_1, out_2):
         )
         load_x(1, 2)
         load_x(2, 4)
+        noise_dealt = tile("noise_dealt", [P, PACK], F32)
+        nc.sync.dma_start(out=noise_dealt[:], in_=nz.rearrange("g (p t) o -> (g p) (t o)", t=PACK))
         nc.scalar.activation(out=warm[:], in_=one[:], func=ACT.Abs_reciprocal_sqrt)
 
         f_grp = [tile("f_grp%d" % s, [P, M, PACK], BF16) for s in range(2)]
@@ -134,111 +135,151 @@ def tile_rows_pl_dft_wiener_kernel(tc, x, fc, fs, nz, out_0, out_1, out_2):
                     )
 
         every = tuple(range(G))
-        stages = [(CH * c, CH, gs) for gs in PAIRS for c in (0, 1)]
-        stages += [(2 * CH, CH, gs) for gs in PAIRS]
-        stages += [(3 * CH, CH - TAIL, every)] if TAIL == 64 else []
-        stages += [(N - TAIL, TAIL, gs) for gs in PAIRS]
-        for n0, wd, gs in stages[:4]:
-            spectra(n0 // CH, gs)
+        for gs in PAIRS:
+            for c in (0, 1):
+                spectra(c, gs)
 
-        blocks = ((0, 2 * CH), (2 * CH, 2 * CH - TAIL), (N - TAIL, TAIL))
-        gain = [tile("gain%d" % h, [P, G, 2 * CH], F32) for h in range(2)]
-        dealt = [tile("dealt%d" % b, [P, PACK, wd], F32) for b, (n0, wd) in enumerate(blocks)]
-        sq = [tile("sq%d" % i, [P, 2, len(gs), wd], F32) for i, (n0, wd, gs) in enumerate(stages)]
-        pw = [tile("pw%d" % i, [P, len(gs), wd], F32) for i, (n0, wd, gs) in enumerate(stages)]
-        rs = [tile("rs%d" % i, [P, len(gs), wd], F32) for i, (n0, wd, gs) in enumerate(stages)]
-        part = [tile("part%d" % i, [P, len(gs), wd], F32) for i, (n0, wd, gs) in enumerate(stages)]
-        out_rows = out_0.rearrange("(g m) n -> m g n", g=G)
+        sq = [[tile("sq%d_%d" % (c, k), [P, 2, 2, CH], F32) for k in range(2)] for c in range(CHUNKS)]
+        pw = [[tile("pw%d_%d" % (c, k), [P, 2, CH], F32) for k in range(2)] for c in range(CHUNKS)]
+        rs = [[tile("rs%d_%d" % (c, k), [P, 2, CH], F32) for k in range(2)] for c in range(CHUNKS)]
+        part = [[tile("part%d_%d" % (c, k), [P, 2, CH], F32) for k in range(2)] for c in range(CHUNKS)]
+        dealt = [tile("dealt%d" % c, [P, PACK, CH], F32) for c in range(CHUNKS)]
+        gain = [tile("gain%d" % c, [P, PACK, CH], F32) for c in range(CHUNKS)]
+        y_grp = [tile("y_grp%d" % c, [P, CH, PACK], BF16) for c in range(CHUNKS)]
+        words = tile("words", [P, N], I32)
+        scales = tile("scales", [P, N], U8)
+        bin_rows = out_0.rearrange("(g m) n -> m g n", g=G)
+        dealt_rows = out_0.rearrange("(q t) n -> q t n", t=PACK)
+        word_rows = out_1.rearrange("v p n t -> (v p) (n t)").bitcast(I32)
+        scale_rows = out_2.rearrange("v f n -> (v f) n").bitcast(I32)
 
-        def squares(i):
-            n0, wd, gs = stages[i]
-            c, lo = divmod(n0, CH)
-            for j, g in enumerate(gs):
+        def deal(c, k, src):
+            for j, g in enumerate(PAIRS[k]):
+                nc.sync.dma_start(out=dealt[c][quadrant(g)], in_=src[:, j, :])
+
+        def squares(c, k):
+            for j, g in enumerate(PAIRS[k]):
+                nc.scalar.activation(out=sq[c][k][:, :, j, :], in_=spec[g][c % 2][:, c // 2], func=ACT.Square)
+
+        def power(c, k):
+            nc.vector.tensor_tensor(out=pw[c][k][:], in0=sq[c][k][:, 0], in1=sq[c][k][:, 1], op=ALU.add)
+            if c in MOVED_AS_POWER:
+                deal(c, k, pw[c][k])
+
+        def first_root(c, k):
+            for j, g in enumerate(PAIRS[k]):
                 nc.scalar.activation(
-                    out=sq[i][:, :, j, :], in_=spec[g][c % 2][:, c // 2, :, lo : lo + wd], func=ACT.Square
-                )
-
-        def power(i):
-            nc.vector.tensor_tensor(out=pw[i][:], in0=sq[i][:, 0], in1=sq[i][:, 1], op=ALU.add)
-
-        def root(i):
-            for j, g in enumerate(stages[i][2]):
-                nc.scalar.activation(
-                    out=rs[i][:, j, :],
-                    in_=pw[i][:, j, :],
+                    out=rs[c][k][:, j, :],
+                    in_=pw[c][k][:, j, :],
                     func=ACT.Abs_reciprocal_sqrt,
                     bias=noise[:, ROWS * g : ROWS * g + 1],
                 )
 
-        def first_product(i):
-            if i in SCALAR_SQUARES:
-                nc.scalar.activation(out=part[i][:], in_=rs[i][:], func=ACT.Square)
-            else:
-                nc.vector.tensor_tensor(out=part[i][:], in0=pw[i][:], in1=rs[i][:], op=ALU.mult)
+        def first_part(c, k):
+            nc.vector.tensor_tensor(out=part[c][k][:], in0=pw[c][k][:], in1=rs[c][k][:], op=ALU.mult)
 
-        def second_product(i):
-            n0, wd, gs = stages[i]
-            h, lo = divmod(n0, 2 * CH)
-            sel = slice(gs[0], G, gs[1] - gs[0])
-            other = pw[i] if i in SCALAR_SQUARES else rs[i]
-            nc.vector.tensor_tensor(out=gain[h][:, sel, lo : lo + wd], in0=part[i][:], in1=other[:], op=ALU.mult)
-            for b, (b0, bw) in enumerate(blocks):
-                if n0 + wd == b0 + bw:
-                    for g in gs:
-                        nc.sync.dma_start(
-                            out=dealt[b][quadrant(g)], in_=gain[h][:, g, b0 % (2 * CH) : b0 % (2 * CH) + bw]
-                        )
-            if n0 == CH:
-                nc.sync.dma_start(out=out_rows[:, sel, 0 : 2 * CH], in_=gain[0][:, sel, :])
+        def first_gain(c, k):
+            nc.vector.tensor_tensor(out=gain[c][:, k::2], in0=part[c][k][:], in1=rs[c][k][:], op=ALU.mult)
+            deal(c, k, gain[c][:, k::2])
 
-        last = len(stages) - 1
-        squares(0)
-        squares(1)
-        power(0)
-        round_x(nc.vector.tensor_copy, 2)
-        power(1)
+        def store_first(c):
+            nc.sync.dma_start(out=bin_rows[:, :, CH * c : CH * (c + 1)], in_=gain[c][:])
+
+        def root(c, k):
+            for j in range(2):
+                t = 2 * k + j
+                nc.scalar.activation(
+                    out=rs[c][k][:, j, :],
+                    in_=dealt[c][:, t, :],
+                    func=ACT.Abs_reciprocal_sqrt,
+                    bias=noise_dealt[:, t : t + 1],
+                )
+
+        def inverse(c, k):
+            nc.scalar.activation(out=part[c][k][:], in_=rs[c][k][:], func=ACT.Square)
+
+        def vpart(c, k):
+            nc.vector.tensor_tensor(out=part[c][k][:], in0=rs[c][k][:], in1=rs[c][k][:], op=ALU.mult)
+
+        def ratio(c, k):
+            ts = slice(2 * k, 2 * k + 2)
+            nc.vector.tensor_tensor(out=gain[c][:, ts], in0=dealt[c][:, ts], in1=part[c][k][:], op=ALU.mult)
+            if k == 1:
+                nc.sync.dma_start(out=dealt_rows[:, :, CH * c : CH * (c + 1)], in_=gain[c][:])
+
+        def round_y(copy, c, lo=0, hi=CH):
+            src = gain[c] if c in MOVED_AS_POWER else dealt[c]
+            interleave(copy, y_grp[c][:, lo:hi], src[:, :, lo:hi])
+
+        def quantise_y(c):
+            cols = slice(CH * c, CH * (c + 1))
+            quantise(nc, words[:, cols], scales[:, cols], y_grp[c][:])
+
+        def store_words(eng, c0, c1):
+            eng.dma_start(out=word_rows[:, CH * c0 : CH * c1], in_=words[:, CH * c0 : CH * c1])
+
+        V, S = nc.vector.tensor_copy, nc.scalar.copy
+        squares(0,0)
+        squares(1,0)
+        power(0,0)
+        round_x(V,2)
+        power(1,0)
+        first_root(0,0)
         quantise_x(2)
-        for i in range(last - 1):
-            root(i)
-            squares(i + 2)
-            first_product(i)
-            if i == 0:
-                round_x(nc.vector.tensor_copy, 3)
-                spectra(2, every)
-            power(i + 2)
-            second_product(i)
-            if i == 0:
-                quantise_x(3)
-            if i == 1:
-                spectra(3, every)
-        root(last - 1)
-        first_product(last - 1)
-        root(last)
-        first_product(last)
-        second_product(last - 1)
-        second_product(last)
-        nc.sync.dma_start(out=out_rows[:, :, 2 * CH :], in_=gain[1][:])
-
-        words = tile("words", [P, N], I32)
-        scales = tile("scales", [P, N], U8)
-        y_grp = [tile("y_grp%d" % b, [P, wd, PACK], BF16) for b, (n0, wd) in enumerate(blocks)]
-        word_rows = out_1.rearrange("v p n t -> (v p) (n t)").bitcast(I32)
-        scale_rows = out_2.rearrange("v f n -> (v f) n").bitcast(I32)
-
-        def quantise_y(b, lo, hi):
-            n0 = blocks[b][0]
-            quantise(nc, words[:, n0 + lo : n0 + hi], scales[:, n0 + lo : n0 + hi], y_grp[b][:, lo:hi])
-
-        interleave(nc.vector.tensor_copy, y_grp[0][:], dealt[0][:])
-        interleave(nc.scalar.copy, y_grp[1][:], dealt[1][:])
-        quantise_y(0, 0, 2 * CH)
-        quantise_y(1, 0, CH)
-        if TAIL < CH:
-            quantise_y(1, CH, 2 * CH - TAIL)
-        nc.sync.dma_start(out=word_rows[:, 0 : N - TAIL], in_=words[:, 0 : N - TAIL])
-        interleave(nc.vector.tensor_copy, y_grp[2][:], dealt[2][:])
-        quantise_y(2, 0, TAIL)
-        nc.scalar.dma_start(out=word_rows[:, N - TAIL :], in_=words[:, N - TAIL :])
+        spectra(2,PAIRS[0])
+        first_part(0,0)
+        squares(0,1)
+        spectra(2,PAIRS[1])
+        round_x(V,3)
+        power(0,1)
+        first_gain(0,0)
+        squares(1,1)
+        quantise_x(3)
+        spectra(3,PAIRS[0])
+        spectra(3,PAIRS[1])
+        power(1,1)
+        first_root(0,1)
+        squares(2,0)
+        first_part(0,1)
+        power(2,0)
+        squares(2,1)
+        first_gain(0,1)
+        power(2,1)
+        store_first(0)
+        squares(3,0)
+        power(3,0)
+        squares(3,1)
+        power(3,1)
+        first_root(3,0)
+        first_root(3,1)
+        root(1,0)
+        first_part(3,0)
+        first_part(3,1)
+        first_gain(3,0)
+        first_gain(3,1)
+        store_first(3)
+        root(1,1)
+        inverse(1,0)
+        inverse(1,1)
+        round_y(V,0)
+        ratio(1,0)
+        quantise_y(0)
+        store_words(nc.sync,0,1)
+        ratio(1,1)
+        root(2,0)
+        root(2,1)
+        inverse(2,0)
+        inverse(2,1)
+        round_y(S,1)
+        ratio(2,0)
+        ratio(2,1)
+        round_y(V,3)
+        round_y(V,2,0,80)
+        round_y(S,2,80,128)
+        quantise_y(1)
+        quantise_y(3)
+        quantise_y(2)
+        store_words(nc.scalar,1,4)
         for q in range(4):
             eng = nc.sync if q % 2 == 0 else nc.scalar
             eng.dma_start(

from contextlib import ExitStack

import concourse.mybir as mybir

G, D, M, N = 4, 128, 128, 512
FLOPS = 2 * 2 * G * D * M * N

F32 = mybir.dt.float32
BF16 = mybir.dt.bfloat16
I32 = mybir.dt.int32
U8 = mybir.dt.uint8
FP8X4 = mybir.dt.float8_e4m3fn_x4
ACT = mybir.ActivationFunctionType
ALU = mybir.AluOpType

P = 128
PACK = 4
ROWS = 32
CH = 128
CHUNKS = N // CH
PAIRS = ((0, 2), (1, 3))
VECTOR_COLS = 80
MOVED_AS_POWER = (1, 2)


def interleave(copy, dst, src):
    copy(
        out=dst.rearrange("p (c i) t -> p c t i", i=4),
        in_=src.rearrange("p t (c i) -> p c t i", i=4),
    )


def quantise(nc, codes, scales, grouped):
    nc.vector.quantize_mx(
        out=codes.bitcast(FP8X4),
        scales=scales,
        in_=grouped.rearrange("p n t -> p (n t)"),
    )


def quadrant(q):
    return slice(ROWS * q, ROWS * (q + 1))


def tile_rows_pl_dft_wiener_kernel(tc, x, fc, fs, nz, out_0, out_1, out_2):
    nc = tc.nc
    with ExitStack() as ctx:
        sb = ctx.enter_context(tc.tile_pool(name="sb", bufs=1))
        psum = ctx.enter_context(tc.psum_pool(name="psum", bufs=1))
        ctx.enter_context(tc.manual_schedule())

        def tile(name, shape, dtype):
            return sb.tile(shape, dtype, name=name, align_bytes=64)

        f_raw = [tile("f_raw%d" % s, [P, PACK, M], F32) for s in range(2)]
        noise_rows = tile("noise_rows", [P, G * ROWS], F32)
        noise = tile("noise", [P, G * ROWS], F32)
        w = tile("w", [P, 2 * M + 2 * M // 4], I32)
        w_codes = w[:, 0 : 2 * M]
        w_scales = w[:, 2 * M :].bitcast(U8)
        one = tile("one", [P, 1], F32)
        warm = tile("warm", [P, 1], F32)
        nc.gpsimd.memset(noise_rows[:], 0.0)
        nc.gpsimd.memset(one[:], 1.0)
        nc.gpsimd.memset(w[:, 2 * M :], 0)
        for s in range(2):
            for q in PAIRS[1]:
                nc.vector.memset(f_raw[s][quadrant(q)], 0.0)

        for eng, f, raw in ((nc.sync, fc, f_raw[0]), (nc.scalar, fs, f_raw[1])):
            for q in PAIRS[0]:
                eng.dma_start(out=raw[quadrant(q)], in_=f.rearrange("(p j) m -> p j m", j=PACK))
        x_rows = x.rearrange("g (p j) n -> (g p) j n", j=PACK)
        x_raw = []

        def load_x(c0, c1):
            t = tile("x_raw%d" % c0, [P, PACK, CH * (c1 - c0)], F32)
            nc.sync.dma_start(out=t[:], in_=x_rows[:, :, CH * c0 : CH * c1])
            x_raw.extend(t[:, :, CH * k : CH * (k + 1)] for k in range(c1 - c0))

        load_x(0, 1)
        nc.sync.dma_start(
            out=noise_rows[0:P:ROWS, :].rearrange("q (g i) -> q g i", g=G),
            in_=nz.rearrange("g (q i) o -> q g (i o)", i=ROWS),
        )
        load_x(1, 2)
        load_x(2, 4)
        noise_dealt = tile("noise_dealt", [P, PACK], F32)
        nc.sync.dma_start(out=noise_dealt[:], in_=nz.rearrange("g (p t) o -> (g p) (t o)", t=PACK))
        nc.scalar.activation(out=warm[:], in_=one[:], func=ACT.Abs_reciprocal_sqrt)

        f_grp = [tile("f_grp%d" % s, [P, M, PACK], BF16) for s in range(2)]
        x_codes = [tile("x_codes%d" % c, [P, CH], I32) for c in range(CHUNKS)]
        x_scales = [tile("x_scales%d" % c, [P, CH], U8) for c in range(CHUNKS)]
        x_grp = [tile("x_grp%d" % c, [P, CH, PACK], BF16) for c in range(CHUNKS)]

        def round_x(copy, c, lo=0, hi=CH):
            interleave(copy, x_grp[c][:, lo:hi], x_raw[c][:, :, lo:hi])

        def quantise_x(c):
            quantise(nc, x_codes[c][:], x_scales[c][:], x_grp[c][:])

        def quantise_f(s):
            cols = slice(M * s, M * (s + 1))
            quantise(nc, w_codes[:, cols], w_scales[:, cols], f_grp[s][:])

        interleave(nc.vector.tensor_copy, f_grp[0][:], f_raw[0][:])
        interleave(nc.scalar.copy, f_grp[1][:], f_raw[1][:])
        quantise_f(0)
        round_x(nc.vector.tensor_copy, 0, 0, VECTOR_COLS)
        round_x(nc.scalar.copy, 0, VECTOR_COLS, CH)
        quantise_f(1)
        quantise_x(0)
        for src, dst in zip(*PAIRS):
            nc.scalar.dma_start(out=w[quadrant(dst), :], in_=w[quadrant(src), :])
        round_x(nc.vector.tensor_copy, 1, 0, VECTOR_COLS)
        round_x(nc.scalar.copy, 1, VECTOR_COLS, CH)
        nc.vector.transpose(out=noise[:], in_=noise_rows[:])
        quantise_x(1)

        spec = [[psum.tile([P, 2, 2, CH], F32, name="spec%d_%d" % (g, b)) for b in range(2)] for g in range(G)]

        def spectra(c, groups):
            for s in range(2):
                for g in groups:
                    cols = slice(M * s, M * (s + 1))
                    nc.tensor.matmul_mx(
                        out=spec[g][c % 2][:, c // 2, s, :],
                        lhsT=w_codes[quadrant(g), cols].bitcast(FP8X4),
                        lhsT_scale=w_scales[quadrant(g), cols],
                        rhs=x_codes[c][quadrant(g), :].bitcast(FP8X4),
                        rhs_scale=x_scales[c][quadrant(g), :],
                        start=True,
                        stop=True,
                    )

        every = tuple(range(G))
        for gs in PAIRS:
            for c in (0, 1):
                spectra(c, gs)

        sq = [[tile("sq%d_%d" % (c, k), [P, 2, 2, CH], F32) for k in range(2)] for c in range(CHUNKS)]
        pw = [[tile("pw%d_%d" % (c, k), [P, 2, CH], F32) for k in range(2)] for c in range(CHUNKS)]
        rs = [[tile("rs%d_%d" % (c, k), [P, 2, CH], F32) for k in range(2)] for c in range(CHUNKS)]
        part = [[tile("part%d_%d" % (c, k), [P, 2, CH], F32) for k in range(2)] for c in range(CHUNKS)]
        dealt = [tile("dealt%d" % c, [P, PACK, CH], F32) for c in range(CHUNKS)]
        gain = [tile("gain%d" % c, [P, PACK, CH], F32) for c in range(CHUNKS)]
        y_grp = [tile("y_grp%d" % c, [P, CH, PACK], BF16) for c in range(CHUNKS)]
        words = tile("words", [P, N], I32)
        scales = tile("scales", [P, N], U8)
        bin_rows = out_0.rearrange("(g m) n -> m g n", g=G)
        dealt_rows = out_0.rearrange("(q t) n -> q t n", t=PACK)
        word_rows = out_1.rearrange("v p n t -> (v p) (n t)").bitcast(I32)
        scale_rows = out_2.rearrange("v f n -> (v f) n").bitcast(I32)

        def deal(c, k, src):
            for j, g in enumerate(PAIRS[k]):
                nc.sync.dma_start(out=dealt[c][quadrant(g)], in_=src[:, j, :])

        def squares(c, k):
            for j, g in enumerate(PAIRS[k]):
                nc.scalar.activation(out=sq[c][k][:, :, j, :], in_=spec[g][c % 2][:, c // 2], func=ACT.Square)

        def power(c, k):
            nc.vector.tensor_tensor(out=pw[c][k][:], in0=sq[c][k][:, 0], in1=sq[c][k][:, 1], op=ALU.add)
            if c in MOVED_AS_POWER:
                deal(c, k, pw[c][k])

        def first_root(c, k):
            for j, g in enumerate(PAIRS[k]):
                nc.scalar.activation(
                    out=rs[c][k][:, j, :],
                    in_=pw[c][k][:, j, :],
                    func=ACT.Abs_reciprocal_sqrt,
                    bias=noise[:, ROWS * g : ROWS * g + 1],
                )

        def first_part(c, k):
            nc.vector.tensor_tensor(out=part[c][k][:], in0=pw[c][k][:], in1=rs[c][k][:], op=ALU.mult)

        def first_gain(c, k):
            nc.vector.tensor_tensor(out=gain[c][:, k::2], in0=part[c][k][:], in1=rs[c][k][:], op=ALU.mult)
            deal(c, k, gain[c][:, k::2])

        def store_first(c):
            nc.sync.dma_start(out=bin_rows[:, :, CH * c : CH * (c + 1)], in_=gain[c][:])

        def root(c, k):
            for j in range(2):
                t = 2 * k + j
                nc.scalar.activation(
                    out=rs[c][k][:, j, :],
                    in_=dealt[c][:, t, :],
                    func=ACT.Abs_reciprocal_sqrt,
                    bias=noise_dealt[:, t : t + 1],
                )

        def inverse(c, k):
            nc.scalar.activation(out=part[c][k][:], in_=rs[c][k][:], func=ACT.Square)

        def vpart(c, k):
            nc.vector.tensor_tensor(out=part[c][k][:], in0=rs[c][k][:], in1=rs[c][k][:], op=ALU.mult)

        def ratio(c, k):
            ts = slice(2 * k, 2 * k + 2)
            nc.vector.tensor_tensor(out=gain[c][:, ts], in0=dealt[c][:, ts], in1=part[c][k][:], op=ALU.mult)
            if k == 1:
                nc.sync.dma_start(out=dealt_rows[:, :, CH * c : CH * (c + 1)], in_=gain[c][:])

        def round_y(copy, c, lo=0, hi=CH):
            src = gain[c] if c in MOVED_AS_POWER else dealt[c]
            interleave(copy, y_grp[c][:, lo:hi], src[:, :, lo:hi])

        def quantise_y(c):
            cols = slice(CH * c, CH * (c + 1))
            quantise(nc, words[:, cols], scales[:, cols], y_grp[c][:])

        def store_words(eng, c0, c1):
            eng.dma_start(out=word_rows[:, CH * c0 : CH * c1], in_=words[:, CH * c0 : CH * c1])

        V, S = nc.vector.tensor_copy, nc.scalar.copy
        squares(0,0)
        squares(1,0)
        power(0,0)
        round_x(V,2)
        power(1,0)
        first_root(0,0)
        quantise_x(2)
        spectra(2,PAIRS[0])
        first_part(0,0)
        squares(0,1)
        spectra(2,PAIRS[1])
        round_x(V,3)
        power(0,1)
        first_gain(0,0)
        squares(1,1)
        quantise_x(3)
        spectra(3,PAIRS[0])
        spectra(3,PAIRS[1])
        power(1,1)
        first_root(0,1)
        squares(2,0)
        first_part(0,1)
        power(2,0)
        squares(2,1)
        first_gain(0,1)
        power(2,1)
        store_first(0)
        squares(3,0)
        power(3,0)
        squares(3,1)
        power(3,1)
        first_root(3,0)
        first_root(3,1)
        root(1,0)
        first_part(3,0)
        first_part(3,1)
        first_gain(3,0)
        first_gain(3,1)
        store_first(3)
        root(1,1)
        inverse(1,0)
        inverse(1,1)
        round_y(V,0)
        ratio(1,0)
        quantise_y(0)
        store_words(nc.sync,0,1)
        ratio(1,1)
        root(2,0)
        root(2,1)
        inverse(2,0)
        inverse(2,1)
        round_y(S,1)
        ratio(2,0)
        ratio(2,1)
        round_y(V,3)
        round_y(V,2,0,80)
        round_y(S,2,80,128)
        quantise_y(1)
        quantise_y(3)
        quantise_y(2)
        store_words(nc.scalar,1,4)
        for q in range(4):
            eng = nc.sync if q % 2 == 0 else nc.scalar
            eng.dma_start(
                out=scale_rows[4 * q : 4 * q + 4, :],
                in_=scales[:].bitcast(I32)[ROWS * q : ROWS * q + 4, :],
            )
